import numpy as np
import ml_dtypes


def mxq(x, axis, fmt="e4m3"):
    dtype, down = {"e4m3": (ml_dtypes.float8_e4m3fn, 7), "e5m2": (ml_dtypes.float8_e5m2, 14)}[fmt]
    v = np.moveaxis(np.asarray(x, np.float32).astype(ml_dtypes.bfloat16).astype(np.float64), axis, -1)
    blocks = v.reshape(v.shape[:-1] + (-1, 32))
    amax = np.abs(blocks).max(-1, keepdims=True)
    byte = np.maximum(np.where(amax > 0, np.frexp(amax)[1] - 1 + 127, 0) - down, 1)
    scale = np.exp2(byte - 127.0)
    codes = (blocks / scale).astype(np.float32).astype(dtype).astype(np.float64)
    return np.moveaxis((codes * scale).reshape(v.shape), -1, axis)


WIDE = False


def mx_kscale(k):
    if not WIDE:
        return np.ones(k)
    levels = np.array([10, -10, 5, -5, 0])
    if k % 512:
        return np.exp2(np.random.permutation(np.resize(levels, k // 32))).repeat(32)
    a = np.empty((k // 512, 16))
    for p in range(k // 512):
        a[p, :8] = np.random.permutation(np.resize(levels, 8))
        for g in range(8):
            far = levels[np.abs(levels - a[p, g]) >= 10]
            a[p, g + 8] = far[np.random.randint(len(far))]
    return np.exp2(a.ravel()).repeat(32)


BF16 = ml_dtypes.bfloat16


def bf(x):
    return np.asarray(x, np.float32).astype(BF16)


def f64(x):
    return np.asarray(x).astype(np.float64)


E2M1 = np.array([0.0, 0.5, 1.0, 1.5, 2.0, 3.0, 4.0, 6.0, -0.0, -0.5, -1.0, -1.5, -2.0, -3.0, -4.0, -6.0])


def pack_weight(w, fmt):
    k, n = w.shape
    w = f64(bf(w)).reshape(k // 32, 32, n)
    amax = np.abs(w).max(1)
    if fmt == "e4m3":
        byte = np.frexp(amax)[1] - 1 + 127 - 7
    else:
        mant, ex = np.frexp(amax / 6.0)
        byte = np.where(mant > 0.5, ex, ex - 1) + 127
    byte = np.clip(np.where(amax > 0, byte, 1), 1, 254)
    scaled = (w * np.exp2(127.0 - byte)[:, None, :]).reshape(k, n).astype(np.float32)
    by_word = np.ascontiguousarray(scaled.reshape(k // 512, 128, 4, n).transpose(0, 1, 3, 2))
    if fmt == "e4m3":
        words = by_word.astype(ml_dtypes.float8_e4m3fn).view(np.uint8)
    else:
        c = by_word.astype(ml_dtypes.float4_e2m1fn).view(np.uint8) & 0xF
        words = c[..., 0::2] | (c[..., 1::2] << 4)
    return np.ascontiguousarray(words), np.ascontiguousarray(byte.astype(np.uint8).reshape(k // 512, 16, n))


def unpack_weight(words, scales, fmt):
    g, p, n, _ = words.shape
    if fmt == "e4m3":
        vals = np.ascontiguousarray(words).view(ml_dtypes.float8_e4m3fn).astype(np.float64)
    else:
        nib = np.empty((g, p, n, 4), np.uint8)
        nib[..., 0::2] = words & 0xF
        nib[..., 1::2] = words >> 4
        vals = E2M1[nib]
    vals = vals * np.repeat(np.exp2(scales.astype(np.float64) - 127.0), 8, axis=1)[..., None]
    return vals.transpose(0, 1, 3, 2).reshape(g * 512, n)
def pack4(w):
    words, scales = pack_weight(w, "e2m1")
    return words.reshape(words.shape[0], 128, -1), scales


def unpack4(words, scales):
    return unpack_weight(words.reshape(words.shape[0], 128, -1, 2), scales, "e2m1")


M, K, J, B = 1024, 1024, 2048, 1024

VOL = 0.6


def setup_inputs():
    s, t = mx_kscale(K), mx_kscale(J)
    factors = VOL * np.random.standard_normal((K, M)) / np.sqrt(K) * s[:, None]
    loadings = np.random.standard_normal((K, J)) / s[:, None]
    f_words, f_scales = pack4(factors)
    l_words, l_scales = pack4(loadings)
    return {"f_words": f_words, "f_scales": f_scales,
            "l_words": l_words, "l_scales": l_scales,
            "base_curve": bf(np.random.uniform(0.3, 1.0, J) * t),
            "cash_flows": bf(np.random.standard_normal((J, B)) / np.sqrt(J) / t[:, None]),
            "accrued": bf(0.5 * np.random.standard_normal(B))}


def reference(f_words, f_scales, l_words, l_scales, base_curve, cash_flows, accrued):
    F = unpack4(f_words, f_scales)
    L = unpack4(l_words, l_scales)
    z = F.T @ L
    d = np.exp(-z) * f64(base_curve)[None, :]
    dirty = mxq(d, 1, "e4m3") @ mxq(f64(cash_flows), 0, "e4m3")
    clean = dirty - f64(accrued)[None, :]
    return clean

@@ -1,0 +1,266 @@
+from contextlib import ExitStack
+
+import concourse.mybir as mybir
+from concourse.masks import make_identity
+
+M, K, J, B = 1024, 1024, 2048, 1024
+FLOPS = 2 * M * K * J + 2 * M * J * B
+
+F32 = mybir.dt.float32
+BF16 = mybir.dt.bfloat16
+I32 = mybir.dt.int32
+U32 = mybir.dt.uint32
+U8 = mybir.dt.uint8
+FP8X4 = mybir.dt.float8_e4m3fn_x4
+FP4X4 = mybir.dt.float4_e2m1fn_x4
+ALU = mybir.AluOpType
+ACT = mybir.ActivationFunctionType
+
+P = 128
+KG = K // 512
+JG = J // 512
+HALF = 512
+MH = M // HALF
+BH = B // HALF
+MT = HALF // P
+
+CF_PLAN = ((0, "V"), (2, "V"), (10, "S"), (15, "S"), (22, "S"), (28, "S"), (32, "S"), (33, "S"))
+SLOTS = 32
+
+
+def tile_factor_curve_bond_book_s4_kernel(
+    tc, f_words, f_scales, l_words, l_scales, base_curve, cash_flows, accrued, out
+):
+    nc = tc.nc
+    with ExitStack() as ctx:
+        keep = ctx.enter_context(tc.tile_pool(name="keep", bufs=1))
+        ebuf = ctx.enter_context(tc.tile_pool(name="ebuf", bufs=3))
+        obuf = ctx.enter_context(tc.tile_pool(name="obuf", bufs=4))
+        psum = ctx.enter_context(tc.psum_pool(name="psum", bufs=4))
+
+        ctx.enter_context(tc.manual_schedule())
+        warm = keep.tile([P, 1], F32, name="warm")
+        nc.gpsimd.memset(warm[:], 0.0)
+        base_rows = keep.tile([P, J // JG], BF16, name="base_rows")
+        nc.gpsimd.memset(base_rows[:], 0.0)
+        f_sc = keep.tile([P, KG, M], U8, name="f_sc", align_bytes=64)
+        l_sc_raw = keep.tile([P, KG, J], U8, name="l_sc_raw", align_bytes=64)
+        nc.vector.memset(f_sc[:].rearrange("p g n -> p (g n)").bitcast(I32), 0)
+        nc.vector.memset(l_sc_raw[:].rearrange("p g n -> p (g n)").bitcast(I32), 0)
+        ident = keep.tile([P, P], BF16, name="ident")
+        make_identity(nc, ident[:])
+
+        nc.scalar.dma_start(out=base_rows[0:JG, :], in_=base_curve.rearrange("(g c) -> g c", g=JG))
+        nc.scalar.activation(out=warm[:], in_=warm[:], func=ACT.Exp)
+
+        f_w = [keep.tile([P, KG, 2 * HALF], U8, name="f_w%d" % h, align_bytes=64) for h in range(MH)]
+        l_raw = [keep.tile([P, KG, 2 * HALF], U8, name="l_raw%d" % g, align_bytes=64) for g in range(JG)]
+
+        def load_f(h):
+            nc.sync.dma_start(
+                out=f_w[h][:], in_=f_words.rearrange("g p c -> p g c")[:, :, 2 * HALF * h : 2 * HALF * (h + 1)]
+            )
+
+        def load_l(g):
+            nc.sync.dma_start(
+                out=l_raw[g][:], in_=l_words.rearrange("g p c -> p g c")[:, :, 2 * HALF * g : 2 * HALF * (g + 1)]
+            )
+
+        load_l(0)
+        load_f(0)
+        for q in range(4):
+            nc.sync.dma_start(
+                out=l_sc_raw[32 * q : 32 * q + 4, :, :].bitcast(I32),
+                in_=l_scales.rearrange("g q n -> q g n")[4 * q : 4 * q + 4].bitcast(I32),
+            )
+        for q in range(4):
+            nc.sync.dma_start(
+                out=f_sc[32 * q : 32 * q + 4, :, :].bitcast(I32),
+                in_=f_scales.rearrange("g q n -> q g n")[4 * q : 4 * q + 4].bitcast(I32),
+            )
+        cf_raw = {}
+
+        def load_cf(g, bh):
+            t_ = keep.tile([P, 4, HALF], BF16, name="cf_raw_%d_%d" % (g, bh), align_bytes=64)
+            cf_raw[g, bh] = t_
+            rows = cash_flows[512 * g : 512 * (g + 1), HALF * bh : HALF * (bh + 1)].rearrange(
+                "(q t i) b -> t q i b", t=4, i=8
+            )
+            for t in range(4):
+                nc.sync.dma_start(out=t_[:, t, :], in_=rows[t])
+
+        load_cf(0, 0)
+        load_l(1)
+        load_cf(1, 0)
+        load_l(2)
+        load_cf(2, 0)
+        load_l(3)
+        load_f(1)
+        load_cf(3, 0)
+        for g in range(JG):
+            load_cf(g, 1)
+        acc_b = keep.tile([P, B], BF16, name="acc_b")
+        nc.sync.dma_start(out=acc_b[:], in_=accrued.partition_broadcast(P))
+
+        base_tqi = keep.tile([P, 4, P], BF16, name="base_tqi")
+        nc.vector.tensor_copy(
+            out=base_tqi[:].rearrange("p t (q i) -> p t q i", i=8),
+            in_=base_rows[:].rearrange("p (q t i) -> p t q i", t=4, i=8),
+        )
+        base_ps = psum.tile([P, 4, P], BF16, name="base_ps", tag="z")
+        for t in range(4):
+            nc.tensor.transpose(base_ps[:, t, :], base_tqi[:, t, :], ident[:])
+        base = keep.tile([P, JG, 4], F32, name="base")
+        nc.vector.tensor_copy(out=base[:].rearrange("p g t -> p t g"), in_=base_ps[:, :, 0:JG])
+
+        l_w = [keep.tile([P, 4, KG, 2 * P], U8, name="l_w%d" % g, align_bytes=64) for g in range(JG)]
+        l_sc = keep.tile([P, 4, KG, HALF], U8, name="l_sc", align_bytes=64)
+
+        def reorder_l(g):
+            nc.vector.tensor_copy(
+                out=l_w[g][:].rearrange("p t k c -> p (t k c)").bitcast(I32).rearrange("p (t k w) -> p t k w", t=4, w=4),
+                in_=l_raw[g][:].rearrange("p k c -> p (k c)").bitcast(I32).rearrange("p (k t w) -> p t k w", t=4, w=4),
+            )
+
+        reorder_l(0)
+        nc.vector.tensor_copy(
+            out=l_sc[:].rearrange("p t k c -> p (t k c)").bitcast(I32).rearrange("p (t k w) -> p t k w", t=4, w=2),
+            in_=l_sc_raw[:].rearrange("p k c -> p (k c)").bitcast(I32).rearrange("p (k t w) -> p t k w", t=4, w=2),
+        )
+
+        e_tiles = {}
+
+        def stage1(h, g, t):
+            if t == 0:
+                e = ebuf.tile([P, 4, HALF], F32, name="e")
+                e_tiles[h, g] = e
+            z = psum.tile([P, HALF], F32, name="z", tag="z")
+            for k in range(KG):
+                nc.tensor.matmul_mx(
+                    out=z[:],
+                    lhsT=l_w[g][:, t, k, :].bitcast(FP4X4),
+                    lhsT_scale=l_sc[:, t, k, P * g : P * (g + 1)],
+                    rhs=f_w[h][:, k, :].bitcast(FP4X4),
+                    rhs_scale=f_sc[:, k, HALF * h : HALF * (h + 1)],
+                    start=(k == 0),
+                    stop=(k == KG - 1),
+                )
+            nc.scalar.activation(out=e_tiles[h, g][:, t, :], in_=z[:], func=ACT.Exp, scale=-1.0)
+
+        d_tiles = {}
+        d_q = {}
+        d_s = {}
+
+        def discount(h, g):
+            d = ebuf.tile([P, HALF, 4], BF16, name="d", align_bytes=64)
+            d_tiles[h, g] = d
+            nc.vector.tensor_tensor(
+                out=d[:].rearrange("p (c i) t -> p c t i", i=4),
+                in0=e_tiles[h, g][:].rearrange("p t (c i) -> p c t i", i=4),
+                in1=base[:, g, :].unsqueeze(1).unsqueeze(3).to_broadcast([P, HALF // 4, 4, 4]),
+                op=ALU.mult,
+            )
+
+        def quantize_d(h, g):
+            d_q[h, g] = keep.tile([P, HALF], U32, name="d_q_%d_%d" % (h, g), align_bytes=64)
+            d_s[h, g] = keep.tile([P, HALF], U8, name="d_s_%d_%d" % (h, g), align_bytes=64)
+            nc.vector.quantize_mx(
+                out=d_q[h, g][:].bitcast(FP8X4),
+                scales=d_s[h, g][:],
+                in_=d_tiles[h, g][:].rearrange("p m t -> p (m t)"),
+            )
+
+        c_tiles = {}
+        c_q = {}
+        c_s = {}
+
+        def interleave_cf(g, bh, engine):
+            c = ebuf.tile([P, HALF, 4], BF16, name="c", align_bytes=64)
+            c_tiles[g, bh] = c
+            dst = c[:].rearrange("p (c i) t -> p c t i", i=4)
+            src = cf_raw[g, bh][:].rearrange("p t (c i) -> p c t i", i=4)
+            if engine == "V":
+                nc.vector.tensor_copy(out=dst, in_=src)
+            else:
+                nc.scalar.copy(out=dst, in_=src)
+
+        def quantize_cf(g, bh):
+            c_q[g, bh] = keep.tile([P, HALF], U32, name="c_q_%d_%d" % (g, bh), align_bytes=64)
+            c_s[g, bh] = keep.tile([P, HALF], U8, name="c_s_%d_%d" % (g, bh), align_bytes=64)
+            nc.vector.quantize_mx(
+                out=c_q[g, bh][:].bitcast(FP8X4),
+                scales=c_s[g, bh][:],
+                in_=c_tiles[g, bh][:].rearrange("p b t -> p (b t)"),
+            )
+
+        def drain(m, bh, acc):
+            o = obuf.tile([P, HALF], F32, name="o")
+            nc.vector.tensor_tensor(out=o[:], in0=acc[:], in1=acc_b[:, HALF * bh : HALF * (bh + 1)], op=ALU.subtract)
+            nc.sync.dma_start(out=out[P * m : P * (m + 1), HALF * bh : HALF * (bh + 1)], in_=o[:])
+
+        ready_d = {}
+        ready_c = {}
+        vector_work = {}
+        for n in range(MH * JG):
+            h, g = divmod(n, JG)
+            vector_work.setdefault(4 * n + 3, []).append((1, discount, (h, g)))
+            vector_work.setdefault(4 * n + 6, []).append((2, quantize_d, (h, g)))
+            ready_d[h, g] = 4 * n + 6 + 4
+        scalar_work = {}
+        for c, (slot, engine) in enumerate(CF_PLAN):
+            bh, g = divmod(c, JG)
+            if engine == "S":
+                scalar_work[slot] = (g, bh)
+            else:
+                vector_work.setdefault(slot, []).append((3, interleave_cf, (g, bh, engine)))
+            done = slot + (5 if engine == "V" else 1)
+            vector_work.setdefault(done, []).append((4, quantize_cf, (g, bh)))
+            ready_c[g, bh] = done + 4
+
+        waiting = [(m, bh) for bh in range(BH) for m in range(M // P)]
+        opened = []
+        spare = 4
+        slot = 0
+        while waiting or opened:
+            if slot < SLOTS:
+                h, g, t = slot // 16, slot // 4 % 4, slot % 4
+                if h == 0 and t == 0 and g + 1 < JG:
+                    reorder_l(g + 1)
+                stage1(h, g, t)
+            if slot in scalar_work:
+                g, bh = scalar_work[slot]
+                interleave_cf(g, bh, "S")
+            for step in range(2 if slot < SLOTS else 4):
+                while waiting and len(opened) < (4 if slot < SLOTS else 8):
+                    m, bh = waiting[0]
+                    if max(ready_d[m // MT, 0], ready_c[0, bh]) > slot:
+                        break
+                    waiting.pop(0)
+                    tag = "o"
+                    if slot >= SLOTS and spare:
+                        tag = "z"
+                        spare -= 1
+                    acc = psum.tile([P, HALF], F32, name="acc", tag=tag)
+                    opened.append([m, bh, 0, acc])
+                for tile_ in opened:
+                    m, bh, g, acc = tile_
+                    if max(ready_d[m // MT, g], ready_c[g, bh]) <= slot:
+                        h = m // MT
+                        cols = slice(P * (m % MT), P * (m % MT + 1))
+                        nc.tensor.matmul_mx(
+                            out=acc[:],
+                            lhsT=d_q[h, g][:, cols].bitcast(FP8X4),
+                            lhsT_scale=d_s[h, g][:, cols],
+                            rhs=c_q[g, bh][:].bitcast(FP8X4),
+                            rhs_scale=c_s[g, bh][:],
+                            start=(g == 0),
+                            stop=(g == JG - 1),
+                        )
+                        tile_[2] += 1
+                        if g == JG - 1:
+                            opened.remove(tile_)
+                            drain(m, bh, acc)
+                        break
+            for kind, work, args in sorted(vector_work.get(slot, []), key=lambda w: w[0]):
+                work(*args)
+            slot += 1

@@ -24,7 +24,7 @@ MH = M // HALF
 BH = B // HALF
 MT = HALF // P
 
-CF_PLAN = ((0, "V"), (2, "V"), (10, "S"), (15, "S"), (22, "S"), (28, "S"), (32, "S"), (33, "S"))
+CF_PLAN = ((2, "V"), (7, "S"), (12, "V"), (15, "S"), (19, "S"), (24, "S"), (27, "S"), (31, "S"))
 SLOTS = 32
 
 
@@ -42,9 +42,9 @@ def tile_factor_curve_bond_book_s4_kernel(
         warm = keep.tile([P, 1], F32, name="warm")
         nc.gpsimd.memset(warm[:], 0.0)
         base_rows = keep.tile([P, J // JG], BF16, name="base_rows")
-        nc.gpsimd.memset(base_rows[:], 0.0)
         f_sc = keep.tile([P, KG, M], U8, name="f_sc", align_bytes=64)
         l_sc_raw = keep.tile([P, KG, J], U8, name="l_sc_raw", align_bytes=64)
+        nc.vector.memset(base_rows[:], 0.0)
         nc.vector.memset(f_sc[:].rearrange("p g n -> p (g n)").bitcast(I32), 0)
         nc.vector.memset(l_sc_raw[:].rearrange("p g n -> p (g n)").bitcast(I32), 0)
         ident = keep.tile([P, P], BF16, name="ident")
@@ -66,18 +66,18 @@ def tile_factor_curve_bond_book_s4_kernel(
                 out=l_raw[g][:], in_=l_words.rearrange("g p c -> p g c")[:, :, 2 * HALF * g : 2 * HALF * (g + 1)]
             )
 
+        def load_scales(tile_, source, quadrants):
+            for q in quadrants:
+                nc.sync.dma_start(
+                    out=tile_[32 * q : 32 * q + 4, :, :].bitcast(I32),
+                    in_=source.rearrange("g q n -> q g n")[4 * q : 4 * q + 4].bitcast(I32),
+                )
+
+        load_scales(f_sc, f_scales, range(4))
         load_l(0)
         load_f(0)
-        for q in range(4):
-            nc.sync.dma_start(
-                out=l_sc_raw[32 * q : 32 * q + 4, :, :].bitcast(I32),
-                in_=l_scales.rearrange("g q n -> q g n")[4 * q : 4 * q + 4].bitcast(I32),
-            )
-        for q in range(4):
-            nc.sync.dma_start(
-                out=f_sc[32 * q : 32 * q + 4, :, :].bitcast(I32),
-                in_=f_scales.rearrange("g q n -> q g n")[4 * q : 4 * q + 4].bitcast(I32),
-            )
+        load_scales(l_sc_raw, l_scales, range(4))
+        load_l(1)
         cf_raw = {}
 
         def load_cf(g, bh):
@@ -90,12 +90,11 @@ def tile_factor_curve_bond_book_s4_kernel(
                 nc.sync.dma_start(out=t_[:, t, :], in_=rows[t])
 
         load_cf(0, 0)
-        load_l(1)
-        load_cf(1, 0)
         load_l(2)
-        load_cf(2, 0)
+        load_cf(1, 0)
         load_l(3)
         load_f(1)
+        load_cf(2, 0)
         load_cf(3, 0)
         for g in range(JG):
             load_cf(g, 1)
@@ -203,9 +202,9 @@ def tile_factor_curve_bond_book_s4_kernel(
         vector_work = {}
         for n in range(MH * JG):
             h, g = divmod(n, JG)
-            vector_work.setdefault(4 * n + 3, []).append((1, discount, (h, g)))
-            vector_work.setdefault(4 * n + 6, []).append((2, quantize_d, (h, g)))
-            ready_d[h, g] = 4 * n + 6 + 4
+            vector_work.setdefault(4 * n + 7, []).append((1, discount, (h, g)))
+            vector_work.setdefault(4 * n + 9, []).append((2, quantize_d, (h, g)))
+            ready_d[h, g] = 4 * n + 9 + 4
         scalar_work = {}
         for c, (slot, engine) in enumerate(CF_PLAN):
             bh, g = divmod(c, JG)
@@ -213,24 +212,25 @@ def tile_factor_curve_bond_book_s4_kernel(
                 scalar_work[slot] = (g, bh)
             else:
                 vector_work.setdefault(slot, []).append((3, interleave_cf, (g, bh, engine)))
-            done = slot + (5 if engine == "V" else 1)
+            done = slot + (4 if engine == "V" else 5)
             vector_work.setdefault(done, []).append((4, quantize_cf, (g, bh)))
             ready_c[g, bh] = done + 4
 
-        waiting = [(m, bh) for bh in range(BH) for m in range(M // P)]
+        for g in range(1, JG):
+            vector_work.setdefault(4 * g - 3, []).append((0, reorder_l, (g,)))
+
+        waiting = [(MT * h + m, bh) for h in range(MH) for bh in range(BH) for m in range(MT)]
         opened = []
         spare = 4
         slot = 0
-        while waiting or opened:
+        while slot <= max(vector_work):
             if slot < SLOTS:
                 h, g, t = slot // 16, slot // 4 % 4, slot % 4
-                if h == 0 and t == 0 and g + 1 < JG:
-                    reorder_l(g + 1)
                 stage1(h, g, t)
             if slot in scalar_work:
                 g, bh = scalar_work[slot]
                 interleave_cf(g, bh, "S")
-            for step in range(2 if slot < SLOTS else 4):
+            for step in range(1 if slot < SLOTS else 4):
                 while waiting and len(opened) < (4 if slot < SLOTS else 8):
                     m, bh = waiting[0]
                     if max(ready_d[m // MT, 0], ready_c[0, bh]) > slot:
@@ -259,8 +259,10 @@ def tile_factor_curve_bond_book_s4_kernel(
                         tile_[2] += 1
                         if g == JG - 1:
                             opened.remove(tile_)
-                            drain(m, bh, acc)
+                            vector_work.setdefault(slot + 2, []).append((-1, drain, (m, bh, acc)))
                         break
             for kind, work, args in sorted(vector_work.get(slot, []), key=lambda w: w[0]):
                 work(*args)
             slot += 1
+            if waiting or opened:
+                vector_work.setdefault(slot, [])

@@ -24,8 +24,13 @@ MH = M // HALF
 BH = B // HALF
 MT = HALF // P
 
-CF_PLAN = ((2, "V"), (7, "S"), (12, "V"), (15, "S"), (19, "S"), (24, "S"), (27, "S"), (31, "S"))
+CF_PLAN = ((3, "V"), (7, "S"), (11, "S"), (15, "S"), (16, "V"), (23, "S"), (27, "S"), (31, "S"))
 SLOTS = 32
+MUL_LAG = 2
+QUANT_LAG = 2
+CF_LAG = {"S": 3, "V": 2}
+READY_LAG = 4
+SHARED_DRAINS = (9, 11, 13)
 
 
 def tile_factor_curve_bond_book_s4_kernel(
@@ -35,85 +40,93 @@ def tile_factor_curve_bond_book_s4_kernel(
     with ExitStack() as ctx:
         keep = ctx.enter_context(tc.tile_pool(name="keep", bufs=1))
         ebuf = ctx.enter_context(tc.tile_pool(name="ebuf", bufs=3))
-        obuf = ctx.enter_context(tc.tile_pool(name="obuf", bufs=4))
+        obuf = ctx.enter_context(tc.tile_pool(name="obuf", bufs=8))
         psum = ctx.enter_context(tc.psum_pool(name="psum", bufs=4))
 
         ctx.enter_context(tc.manual_schedule())
-        warm = keep.tile([P, 1], F32, name="warm")
-        nc.gpsimd.memset(warm[:], 0.0)
-        base_rows = keep.tile([P, J // JG], BF16, name="base_rows")
-        f_sc = keep.tile([P, KG, M], U8, name="f_sc", align_bytes=64)
-        l_sc_raw = keep.tile([P, KG, J], U8, name="l_sc_raw", align_bytes=64)
-        nc.vector.memset(base_rows[:], 0.0)
-        nc.vector.memset(f_sc[:].rearrange("p g n -> p (g n)").bitcast(I32), 0)
-        nc.vector.memset(l_sc_raw[:].rearrange("p g n -> p (g n)").bitcast(I32), 0)
-        ident = keep.tile([P, P], BF16, name="ident")
-        make_identity(nc, ident[:])
-
-        nc.scalar.dma_start(out=base_rows[0:JG, :], in_=base_curve.rearrange("(g c) -> g c", g=JG))
-        nc.scalar.activation(out=warm[:], in_=warm[:], func=ACT.Exp)
 
         f_w = [keep.tile([P, KG, 2 * HALF], U8, name="f_w%d" % h, align_bytes=64) for h in range(MH)]
         l_raw = [keep.tile([P, KG, 2 * HALF], U8, name="l_raw%d" % g, align_bytes=64) for g in range(JG)]
+        f_sc = keep.tile([P, KG, M], U8, name="f_sc", align_bytes=64)
+        l_sc_raw = keep.tile([P, KG, J], U8, name="l_sc_raw", align_bytes=64)
+        rows = keep.tile([P, HALF + P], BF16, name="rows")
+        ident = keep.tile([P, P], BF16, name="ident")
+        warm = keep.tile([P, 1], F32, name="warm")
 
-        def load_f(h):
+        def load_words(tile_, words, i):
             nc.sync.dma_start(
-                out=f_w[h][:], in_=f_words.rearrange("g p c -> p g c")[:, :, 2 * HALF * h : 2 * HALF * (h + 1)]
+                out=tile_[:], in_=words.rearrange("g p c -> p g c")[:, :, 2 * HALF * i : 2 * HALF * (i + 1)]
             )
 
-        def load_l(g):
-            nc.sync.dma_start(
-                out=l_raw[g][:], in_=l_words.rearrange("g p c -> p g c")[:, :, 2 * HALF * g : 2 * HALF * (g + 1)]
-            )
-
-        def load_scales(tile_, source, quadrants):
-            for q in quadrants:
+        def load_scales(tile_, source):
+            for q in range(4):
                 nc.sync.dma_start(
                     out=tile_[32 * q : 32 * q + 4, :, :].bitcast(I32),
                     in_=source.rearrange("g q n -> q g n")[4 * q : 4 * q + 4].bitcast(I32),
                 )
 
-        load_scales(f_sc, f_scales, range(4))
-        load_l(0)
-        load_f(0)
-        load_scales(l_sc_raw, l_scales, range(4))
-        load_l(1)
         cf_raw = {}
 
         def load_cf(g, bh):
-            t_ = keep.tile([P, 4, HALF], BF16, name="cf_raw_%d_%d" % (g, bh), align_bytes=64)
-            cf_raw[g, bh] = t_
-            rows = cash_flows[512 * g : 512 * (g + 1), HALF * bh : HALF * (bh + 1)].rearrange(
+            cf_raw[g, bh] = keep.tile([P, 4, HALF], BF16, name="cf_raw_%d_%d" % (g, bh), align_bytes=64)
+            source = cash_flows[512 * g : 512 * (g + 1), HALF * bh : HALF * (bh + 1)].rearrange(
                 "(q t i) b -> t q i b", t=4, i=8
             )
             for t in range(4):
-                nc.sync.dma_start(out=t_[:, t, :], in_=rows[t])
+                nc.sync.dma_start(out=cf_raw[g, bh][:, t, :], in_=source[t])
 
+        nc.gpsimd.memset(warm[:], 0.0)
+        nc.vector.memset(rows[:], 0.0)
+        nc.vector.memset(l_sc_raw[:].rearrange("p g n -> p (g n)").bitcast(I32), 0)
+        nc.vector.memset(f_sc[:].rearrange("p g n -> p (g n)").bitcast(I32), 0)
+        nc.scalar.dma_start(out=rows[0:JG, 0:HALF], in_=base_curve.rearrange("(g c) -> g c", g=JG))
+        nc.scalar.dma_start(out=rows[0 : B // P, HALF : HALF + P], in_=accrued.rearrange("(r c) -> r c", c=P))
+        make_identity(nc, ident[:])
+        nc.scalar.activation(out=warm[:], in_=warm[:], func=ACT.Exp)
+        load_scales(l_sc_raw, l_scales)
+        load_words(l_raw[0], l_words, 0)
+        load_words(f_w[0], f_words, 0)
+        load_scales(f_sc, f_scales)
+        load_words(l_raw[1], l_words, 1)
         load_cf(0, 0)
-        load_l(2)
+        load_words(l_raw[2], l_words, 2)
         load_cf(1, 0)
-        load_l(3)
-        load_f(1)
+        load_words(l_raw[3], l_words, 3)
+        load_words(f_w[1], f_words, 1)
         load_cf(2, 0)
         load_cf(3, 0)
         for g in range(JG):
             load_cf(g, 1)
-        acc_b = keep.tile([P, B], BF16, name="acc_b")
-        nc.sync.dma_start(out=acc_b[:], in_=accrued.partition_broadcast(P))
 
-        base_tqi = keep.tile([P, 4, P], BF16, name="base_tqi")
-        nc.vector.tensor_copy(
-            out=base_tqi[:].rearrange("p t (q i) -> p t q i", i=8),
-            in_=base_rows[:].rearrange("p (q t i) -> p t q i", t=4, i=8),
-        )
-        base_ps = psum.tile([P, 4, P], BF16, name="base_ps", tag="z")
-        for t in range(4):
-            nc.tensor.transpose(base_ps[:, t, :], base_tqi[:, t, :], ident[:])
+        turned = keep.tile([P, 5, P], BF16, name="turned")
         base = keep.tile([P, JG, 4], F32, name="base")
-        nc.vector.tensor_copy(out=base[:].rearrange("p g t -> p t g"), in_=base_ps[:, :, 0:JG])
+        acc_col = keep.tile([P, B // P], BF16, name="acc_col")
+        acc_b = keep.tile([P, B], BF16, name="acc_b")
+
+        def order_rows():
+            nc.vector.tensor_copy(
+                out=turned[:, 0:4, :].rearrange("p t (q i) -> p t q i", i=8),
+                in_=rows[:, 0:HALF].rearrange("p (q t i) -> p t q i", t=4, i=8),
+            )
+            nc.vector.tensor_copy(out=turned[:, 4, :], in_=rows[:, HALF : HALF + P])
+
+        def turn_rows():
+            columns_ps = psum.tile([P, 5, P], BF16, name="columns_ps", tag="o")
+            for t in range(5):
+                nc.tensor.transpose(columns_ps[:, t, :], turned[:, t, :], ident[:])
+            nc.vector.tensor_copy(out=base[:].rearrange("p g t -> p t g"), in_=columns_ps[:, 0:4, 0:JG])
+            nc.vector.tensor_copy(out=acc_col[:], in_=columns_ps[:, 4, 0 : B // P])
+
+        def spread_accrued():
+            spread_ps = psum.tile([P, B], BF16, name="spread_ps", tag="o")
+            for r in range(B // P):
+                nc.tensor.transpose(
+                    spread_ps[:, P * r : P * (r + 1)], acc_col[:, r : r + 1].to_broadcast([P, P]), ident[:]
+                )
+            nc.scalar.copy(out=acc_b[:], in_=spread_ps[:])
 
         l_w = [keep.tile([P, 4, KG, 2 * P], U8, name="l_w%d" % g, align_bytes=64) for g in range(JG)]
-        l_sc = keep.tile([P, 4, KG, HALF], U8, name="l_sc", align_bytes=64)
+        l_sc = keep.tile([P, 4, KG, J // 4], U8, name="l_sc", align_bytes=64)
 
         def reorder_l(g):
             nc.vector.tensor_copy(
@@ -121,6 +134,9 @@ def tile_factor_curve_bond_book_s4_kernel(
                 in_=l_raw[g][:].rearrange("p k c -> p (k c)").bitcast(I32).rearrange("p (k t w) -> p t k w", t=4, w=4),
             )
 
+        order_rows()
+        turn_rows()
+        spread_accrued()
         reorder_l(0)
         nc.vector.tensor_copy(
             out=l_sc[:].rearrange("p t k c -> p (t k c)").bitcast(I32).rearrange("p (t k w) -> p t k w", t=4, w=2),
@@ -129,34 +145,45 @@ def tile_factor_curve_bond_book_s4_kernel(
 
         e_tiles = {}
 
-        def stage1(h, g, t):
-            if t == 0:
-                e = ebuf.tile([P, 4, HALF], F32, name="e")
-                e_tiles[h, g] = e
+        def stage1(h, g, s):
+            if s == 0:
+                e_tiles[h, g] = ebuf.tile([P, 4, HALF], F32, name="e")
             z = psum.tile([P, HALF], F32, name="z", tag="z")
-            for k in range(KG):
-                nc.tensor.matmul_mx(
-                    out=z[:],
-                    lhsT=l_w[g][:, t, k, :].bitcast(FP4X4),
-                    lhsT_scale=l_sc[:, t, k, P * g : P * (g + 1)],
-                    rhs=f_w[h][:, k, :].bitcast(FP4X4),
-                    rhs_scale=f_sc[:, k, HALF * h : HALF * (h + 1)],
-                    start=(k == 0),
-                    stop=(k == KG - 1),
-                )
-            nc.scalar.activation(out=e_tiles[h, g][:, t, :], in_=z[:], func=ACT.Exp, scale=-1.0)
+            halves = h == 0 and g == 0
+            if halves:
+                parts = [(2 * (s % 2) + j, HALF // 2 * (s // 2), HALF // 2) for j in range(2)]
+            else:
+                parts = [(s, 0, HALF)]
+            for j, (t, m0, width) in enumerate(parts):
+                for k in range(KG):
+                    nc.tensor.matmul_mx(
+                        out=z[:, width * j : width * (j + 1)],
+                        lhsT=l_w[g][:, t, k, :].bitcast(FP4X4),
+                        lhsT_scale=l_sc[:, t, k, P * g : P * (g + 1)],
+                        rhs=f_w[h][:, k, 2 * m0 : 2 * (m0 + width)].bitcast(FP4X4),
+                        rhs_scale=f_sc[:, k, HALF * h + m0 : HALF * h + m0 + width],
+                        start=(k == 0),
+                        stop=(k == KG - 1),
+                    )
+            t, m0, width = parts[0]
+            nc.scalar.activation(
+                out=e_tiles[h, g][:, t : t + len(parts), m0 : m0 + width],
+                in_=z[:].rearrange("p (j m) -> p j m", j=len(parts)),
+                func=ACT.Exp,
+                scale=-1.0,
+            )
 
         d_tiles = {}
         d_q = {}
         d_s = {}
 
-        def discount(h, g):
-            d = ebuf.tile([P, HALF, 4], BF16, name="d", align_bytes=64)
-            d_tiles[h, g] = d
+        def discount(h, g, m0, width):
+            if m0 == 0:
+                d_tiles[h, g] = ebuf.tile([P, HALF, 4], BF16, name="d", align_bytes=64)
             nc.vector.tensor_tensor(
-                out=d[:].rearrange("p (c i) t -> p c t i", i=4),
-                in0=e_tiles[h, g][:].rearrange("p t (c i) -> p c t i", i=4),
-                in1=base[:, g, :].unsqueeze(1).unsqueeze(3).to_broadcast([P, HALF // 4, 4, 4]),
+                out=d_tiles[h, g][:, m0 : m0 + width, :].rearrange("p (c i) t -> p c t i", i=4),
+                in0=e_tiles[h, g][:, :, m0 : m0 + width].rearrange("p t (c i) -> p c t i", i=4),
+                in1=base[:, g, :].unsqueeze(1).unsqueeze(3).to_broadcast([P, width // 4, 4, 4]),
                 op=ALU.mult,
             )
 
@@ -174,9 +201,8 @@ def tile_factor_curve_bond_book_s4_kernel(
         c_s = {}
 
         def interleave_cf(g, bh, engine):
-            c = ebuf.tile([P, HALF, 4], BF16, name="c", align_bytes=64)
-            c_tiles[g, bh] = c
-            dst = c[:].rearrange("p (c i) t -> p c t i", i=4)
+            c_tiles[g, bh] = ebuf.tile([P, HALF, 4], BF16, name="c", align_bytes=64)
+            dst = c_tiles[g, bh][:].rearrange("p (c i) t -> p c t i", i=4)
             src = cf_raw[g, bh][:].rearrange("p t (c i) -> p c t i", i=4)
             if engine == "V":
                 nc.vector.tensor_copy(out=dst, in_=src)
@@ -192,41 +218,60 @@ def tile_factor_curve_bond_book_s4_kernel(
                 in_=c_tiles[g, bh][:].rearrange("p b t -> p (b t)"),
             )
 
-        def drain(m, bh, acc):
-            o = obuf.tile([P, HALF], F32, name="o")
-            nc.vector.tensor_tensor(out=o[:], in0=acc[:], in1=acc_b[:, HALF * bh : HALF * (bh + 1)], op=ALU.subtract)
+        def store(m, bh, o):
             nc.sync.dma_start(out=out[P * m : P * (m + 1), HALF * bh : HALF * (bh + 1)], in_=o[:])
+
+        def drain(m, bh, acc, shared):
+            o = obuf.tile([P, HALF], F32, name="o")
+            owed = acc_b[:, HALF * bh : HALF * (bh + 1)]
+            if shared:
+                dirty = obuf.tile([P, HALF], F32, name="dirty")
+                nc.scalar.copy(out=dirty[:], in_=acc[:])
+                nc.gpsimd.tensor_tensor(out=o[:], in0=dirty[:], in1=owed, op=ALU.subtract)
+            else:
+                nc.vector.tensor_tensor(out=o[:], in0=acc[:], in1=owed, op=ALU.subtract)
+            if shared:
+                at(slot + 2, 9, store, m, bh, o)
+            else:
+                store(m, bh, o)
 
         ready_d = {}
         ready_c = {}
         vector_work = {}
+
+        def at(slot, rank, work, *args):
+            vector_work.setdefault(slot, []).append((rank, work, args))
+
         for n in range(MH * JG):
             h, g = divmod(n, JG)
-            vector_work.setdefault(4 * n + 7, []).append((1, discount, (h, g)))
-            vector_work.setdefault(4 * n + 9, []).append((2, quantize_d, (h, g)))
-            ready_d[h, g] = 4 * n + 9 + 4
+            last = 4 * n + 3
+            if n == 0:
+                at(1 + MUL_LAG, 1, discount, h, g, 0, HALF // 2)
+                at(3 + MUL_LAG, 1, discount, h, g, HALF // 2, HALF // 2)
+            else:
+                at(last + MUL_LAG, 1, discount, h, g, 0, HALF)
+            at(last + MUL_LAG + QUANT_LAG, 2, quantize_d, h, g)
+            ready_d[h, g] = last + MUL_LAG + QUANT_LAG + READY_LAG
         scalar_work = {}
         for c, (slot, engine) in enumerate(CF_PLAN):
             bh, g = divmod(c, JG)
             if engine == "S":
                 scalar_work[slot] = (g, bh)
             else:
-                vector_work.setdefault(slot, []).append((3, interleave_cf, (g, bh, engine)))
-            done = slot + (4 if engine == "V" else 5)
-            vector_work.setdefault(done, []).append((4, quantize_cf, (g, bh)))
-            ready_c[g, bh] = done + 4
-
+                at(slot, 3, interleave_cf, g, bh, engine)
+            at(slot + CF_LAG[engine], 4, quantize_cf, g, bh)
+            ready_c[g, bh] = slot + CF_LAG[engine] + READY_LAG
         for g in range(1, JG):
-            vector_work.setdefault(4 * g - 3, []).append((0, reorder_l, (g,)))
+            at(4 * g - 3, 0, reorder_l, g)
 
         waiting = [(MT * h + m, bh) for h in range(MH) for bh in range(BH) for m in range(MT)]
         opened = []
         spare = 4
+        closed = 0
         slot = 0
-        while slot <= max(vector_work):
+        while slot < SLOTS or waiting or opened or slot <= max(vector_work):
             if slot < SLOTS:
-                h, g, t = slot // 16, slot // 4 % 4, slot % 4
-                stage1(h, g, t)
+                stage1(slot // 16, slot // 4 % 4, slot % 4)
             if slot in scalar_work:
                 g, bh = scalar_work[slot]
                 interleave_cf(g, bh, "S")
@@ -244,8 +289,8 @@ def tile_factor_curve_bond_book_s4_kernel(
                     opened.append([m, bh, 0, acc])
                 for tile_ in opened:
                     m, bh, g, acc = tile_
-                    if max(ready_d[m // MT, g], ready_c[g, bh]) <= slot:
-                        h = m // MT
+                    h = m // MT
+                    if max(ready_d[h, g], ready_c[g, bh]) <= slot:
                         cols = slice(P * (m % MT), P * (m % MT + 1))
                         nc.tensor.matmul_mx(
                             out=acc[:],
@@ -259,10 +304,9 @@ def tile_factor_curve_bond_book_s4_kernel(
                         tile_[2] += 1
                         if g == JG - 1:
                             opened.remove(tile_)
-                            vector_work.setdefault(slot + 2, []).append((-1, drain, (m, bh, acc)))
+                            at(slot, -2, drain, m, bh, acc, closed in SHARED_DRAINS)
+                            closed += 1
                         break
-            for kind, work, args in sorted(vector_work.get(slot, []), key=lambda w: w[0]):
+            for rank, work, args in sorted(vector_work.get(slot, []), key=lambda w: w[0]):
                 work(*args)
             slot += 1
-            if waiting or opened:
-                vector_work.setdefault(slot, [])

from contextlib import ExitStack

import concourse.mybir as mybir
from concourse.masks import make_identity

M, K, J, B = 1024, 1024, 2048, 1024
FLOPS = 2 * M * K * J + 2 * M * J * B

F32 = mybir.dt.float32
BF16 = mybir.dt.bfloat16
I32 = mybir.dt.int32
U32 = mybir.dt.uint32
U8 = mybir.dt.uint8
FP8X4 = mybir.dt.float8_e4m3fn_x4
FP4X4 = mybir.dt.float4_e2m1fn_x4
ALU = mybir.AluOpType
ACT = mybir.ActivationFunctionType

P = 128
KG = K // 512
JG = J // 512
HALF = 512
MH = M // HALF
BH = B // HALF
MT = HALF // P

CF_PLAN = ((3, "V"), (7, "S"), (11, "S"), (15, "S"), (16, "V"), (23, "S"), (27, "S"), (31, "S"))
SLOTS = 32
MUL_LAG = 2
QUANT_LAG = 2
CF_LAG = {"S": 3, "V": 2}
READY_LAG = 4
SHARED_DRAINS = (9, 11, 13)


def tile_factor_curve_bond_book_s4_kernel(
    tc, f_words, f_scales, l_words, l_scales, base_curve, cash_flows, accrued, out
):
    nc = tc.nc
    with ExitStack() as ctx:
        keep = ctx.enter_context(tc.tile_pool(name="keep", bufs=1))
        ebuf = ctx.enter_context(tc.tile_pool(name="ebuf", bufs=3))
        obuf = ctx.enter_context(tc.tile_pool(name="obuf", bufs=8))
        psum = ctx.enter_context(tc.psum_pool(name="psum", bufs=4))

        ctx.enter_context(tc.manual_schedule())

        f_w = [keep.tile([P, KG, 2 * HALF], U8, name="f_w%d" % h, align_bytes=64) for h in range(MH)]
        l_raw = [keep.tile([P, KG, 2 * HALF], U8, name="l_raw%d" % g, align_bytes=64) for g in range(JG)]
        f_sc = keep.tile([P, KG, M], U8, name="f_sc", align_bytes=64)
        l_sc_raw = keep.tile([P, KG, J], U8, name="l_sc_raw", align_bytes=64)
        rows = keep.tile([P, HALF + P], BF16, name="rows")
        ident = keep.tile([P, P], BF16, name="ident")
        warm = keep.tile([P, 1], F32, name="warm")

        def load_words(tile_, words, i):
            nc.sync.dma_start(
                out=tile_[:], in_=words.rearrange("g p c -> p g c")[:, :, 2 * HALF * i : 2 * HALF * (i + 1)]
            )

        def load_scales(tile_, source):
            for q in range(4):
                nc.sync.dma_start(
                    out=tile_[32 * q : 32 * q + 4, :, :].bitcast(I32),
                    in_=source.rearrange("g q n -> q g n")[4 * q : 4 * q + 4].bitcast(I32),
                )

        cf_raw = {}

        def load_cf(g, bh):
            cf_raw[g, bh] = keep.tile([P, 4, HALF], BF16, name="cf_raw_%d_%d" % (g, bh), align_bytes=64)
            source = cash_flows[512 * g : 512 * (g + 1), HALF * bh : HALF * (bh + 1)].rearrange(
                "(q t i) b -> t q i b", t=4, i=8
            )
            for t in range(4):
                nc.sync.dma_start(out=cf_raw[g, bh][:, t, :], in_=source[t])

        nc.gpsimd.memset(warm[:], 0.0)
        nc.vector.memset(rows[:], 0.0)
        nc.vector.memset(l_sc_raw[:].rearrange("p g n -> p (g n)").bitcast(I32), 0)
        nc.vector.memset(f_sc[:].rearrange("p g n -> p (g n)").bitcast(I32), 0)
        nc.scalar.dma_start(out=rows[0:JG, 0:HALF], in_=base_curve.rearrange("(g c) -> g c", g=JG))
        nc.scalar.dma_start(out=rows[0 : B // P, HALF : HALF + P], in_=accrued.rearrange("(r c) -> r c", c=P))
        make_identity(nc, ident[:])
        nc.scalar.activation(out=warm[:], in_=warm[:], func=ACT.Exp)
        load_scales(l_sc_raw, l_scales)
        load_words(l_raw[0], l_words, 0)
        load_words(f_w[0], f_words, 0)
        load_scales(f_sc, f_scales)
        load_words(l_raw[1], l_words, 1)
        load_cf(0, 0)
        load_words(l_raw[2], l_words, 2)
        load_cf(1, 0)
        load_words(l_raw[3], l_words, 3)
        load_words(f_w[1], f_words, 1)
        load_cf(2, 0)
        load_cf(3, 0)
        for g in range(JG):
            load_cf(g, 1)

        turned = keep.tile([P, 5, P], BF16, name="turned")
        base = keep.tile([P, JG, 4], F32, name="base")
        acc_col = keep.tile([P, B // P], BF16, name="acc_col")
        acc_b = keep.tile([P, B], BF16, name="acc_b")

        def order_rows():
            nc.vector.tensor_copy(
                out=turned[:, 0:4, :].rearrange("p t (q i) -> p t q i", i=8),
                in_=rows[:, 0:HALF].rearrange("p (q t i) -> p t q i", t=4, i=8),
            )
            nc.vector.tensor_copy(out=turned[:, 4, :], in_=rows[:, HALF : HALF + P])

        def turn_rows():
            columns_ps = psum.tile([P, 5, P], BF16, name="columns_ps", tag="o")
            for t in range(5):
                nc.tensor.transpose(columns_ps[:, t, :], turned[:, t, :], ident[:])
            nc.vector.tensor_copy(out=base[:].rearrange("p g t -> p t g"), in_=columns_ps[:, 0:4, 0:JG])
            nc.vector.tensor_copy(out=acc_col[:], in_=columns_ps[:, 4, 0 : B // P])

        def spread_accrued():
            spread_ps = psum.tile([P, B], BF16, name="spread_ps", tag="o")
            for r in range(B // P):
                nc.tensor.transpose(
                    spread_ps[:, P * r : P * (r + 1)], acc_col[:, r : r + 1].to_broadcast([P, P]), ident[:]
                )
            nc.scalar.copy(out=acc_b[:], in_=spread_ps[:])

        l_w = [keep.tile([P, 4, KG, 2 * P], U8, name="l_w%d" % g, align_bytes=64) for g in range(JG)]
        l_sc = keep.tile([P, 4, KG, J // 4], U8, name="l_sc", align_bytes=64)

        def reorder_l(g):
            nc.vector.tensor_copy(
                out=l_w[g][:].rearrange("p t k c -> p (t k c)").bitcast(I32).rearrange("p (t k w) -> p t k w", t=4, w=4),
                in_=l_raw[g][:].rearrange("p k c -> p (k c)").bitcast(I32).rearrange("p (k t w) -> p t k w", t=4, w=4),
            )

        order_rows()
        turn_rows()
        spread_accrued()
        reorder_l(0)
        nc.vector.tensor_copy(
            out=l_sc[:].rearrange("p t k c -> p (t k c)").bitcast(I32).rearrange("p (t k w) -> p t k w", t=4, w=2),
            in_=l_sc_raw[:].rearrange("p k c -> p (k c)").bitcast(I32).rearrange("p (k t w) -> p t k w", t=4, w=2),
        )

        e_tiles = {}

        def stage1(h, g, s):
            if s == 0:
                e_tiles[h, g] = ebuf.tile([P, 4, HALF], F32, name="e")
            z = psum.tile([P, HALF], F32, name="z", tag="z")
            halves = h == 0 and g == 0
            if halves:
                parts = [(2 * (s % 2) + j, HALF // 2 * (s // 2), HALF // 2) for j in range(2)]
            else:
                parts = [(s, 0, HALF)]
            for j, (t, m0, width) in enumerate(parts):
                for k in range(KG):
                    nc.tensor.matmul_mx(
                        out=z[:, width * j : width * (j + 1)],
                        lhsT=l_w[g][:, t, k, :].bitcast(FP4X4),
                        lhsT_scale=l_sc[:, t, k, P * g : P * (g + 1)],
                        rhs=f_w[h][:, k, 2 * m0 : 2 * (m0 + width)].bitcast(FP4X4),
                        rhs_scale=f_sc[:, k, HALF * h + m0 : HALF * h + m0 + width],
                        start=(k == 0),
                        stop=(k == KG - 1),
                    )
            t, m0, width = parts[0]
            nc.scalar.activation(
                out=e_tiles[h, g][:, t : t + len(parts), m0 : m0 + width],
                in_=z[:].rearrange("p (j m) -> p j m", j=len(parts)),
                func=ACT.Exp,
                scale=-1.0,
            )

        d_tiles = {}
        d_q = {}
        d_s = {}

        def discount(h, g, m0, width):
            if m0 == 0:
                d_tiles[h, g] = ebuf.tile([P, HALF, 4], BF16, name="d", align_bytes=64)
            nc.vector.tensor_tensor(
                out=d_tiles[h, g][:, m0 : m0 + width, :].rearrange("p (c i) t -> p c t i", i=4),
                in0=e_tiles[h, g][:, :, m0 : m0 + width].rearrange("p t (c i) -> p c t i", i=4),
                in1=base[:, g, :].unsqueeze(1).unsqueeze(3).to_broadcast([P, width // 4, 4, 4]),
                op=ALU.mult,
            )

        def quantize_d(h, g):
            d_q[h, g] = keep.tile([P, HALF], U32, name="d_q_%d_%d" % (h, g), align_bytes=64)
            d_s[h, g] = keep.tile([P, HALF], U8, name="d_s_%d_%d" % (h, g), align_bytes=64)
            nc.vector.quantize_mx(
                out=d_q[h, g][:].bitcast(FP8X4),
                scales=d_s[h, g][:],
                in_=d_tiles[h, g][:].rearrange("p m t -> p (m t)"),
            )

        c_tiles = {}
        c_q = {}
        c_s = {}

        def interleave_cf(g, bh, engine):
            c_tiles[g, bh] = ebuf.tile([P, HALF, 4], BF16, name="c", align_bytes=64)
            dst = c_tiles[g, bh][:].rearrange("p (c i) t -> p c t i", i=4)
            src = cf_raw[g, bh][:].rearrange("p t (c i) -> p c t i", i=4)
            if engine == "V":
                nc.vector.tensor_copy(out=dst, in_=src)
            else:
                nc.scalar.copy(out=dst, in_=src)

        def quantize_cf(g, bh):
            c_q[g, bh] = keep.tile([P, HALF], U32, name="c_q_%d_%d" % (g, bh), align_bytes=64)
            c_s[g, bh] = keep.tile([P, HALF], U8, name="c_s_%d_%d" % (g, bh), align_bytes=64)
            nc.vector.quantize_mx(
                out=c_q[g, bh][:].bitcast(FP8X4),
                scales=c_s[g, bh][:],
                in_=c_tiles[g, bh][:].rearrange("p b t -> p (b t)"),
            )

        def store(m, bh, o):
            nc.sync.dma_start(out=out[P * m : P * (m + 1), HALF * bh : HALF * (bh + 1)], in_=o[:])

        def drain(m, bh, acc, shared):
            o = obuf.tile([P, HALF], F32, name="o")
            owed = acc_b[:, HALF * bh : HALF * (bh + 1)]
            if shared:
                dirty = obuf.tile([P, HALF], F32, name="dirty")
                nc.scalar.copy(out=dirty[:], in_=acc[:])
                nc.gpsimd.tensor_tensor(out=o[:], in0=dirty[:], in1=owed, op=ALU.subtract)
            else:
                nc.vector.tensor_tensor(out=o[:], in0=acc[:], in1=owed, op=ALU.subtract)
            if shared:
                at(slot + 2, 9, store, m, bh, o)
            else:
                store(m, bh, o)

        ready_d = {}
        ready_c = {}
        vector_work = {}

        def at(slot, rank, work, *args):
            vector_work.setdefault(slot, []).append((rank, work, args))

        for n in range(MH * JG):
            h, g = divmod(n, JG)
            last = 4 * n + 3
            if n == 0:
                at(1 + MUL_LAG, 1, discount, h, g, 0, HALF // 2)
                at(3 + MUL_LAG, 1, discount, h, g, HALF // 2, HALF // 2)
            else:
                at(last + MUL_LAG, 1, discount, h, g, 0, HALF)
            at(last + MUL_LAG + QUANT_LAG, 2, quantize_d, h, g)
            ready_d[h, g] = last + MUL_LAG + QUANT_LAG + READY_LAG
        scalar_work = {}
        for c, (slot, engine) in enumerate(CF_PLAN):
            bh, g = divmod(c, JG)
            if engine == "S":
                scalar_work[slot] = (g, bh)
            else:
                at(slot, 3, interleave_cf, g, bh, engine)
            at(slot + CF_LAG[engine], 4, quantize_cf, g, bh)
            ready_c[g, bh] = slot + CF_LAG[engine] + READY_LAG
        for g in range(1, JG):
            at(4 * g - 3, 0, reorder_l, g)

        waiting = [(MT * h + m, bh) for h in range(MH) for bh in range(BH) for m in range(MT)]
        opened = []
        spare = 4
        closed = 0
        slot = 0
        while slot < SLOTS or waiting or opened or slot <= max(vector_work):
            if slot < SLOTS:
                stage1(slot // 16, slot // 4 % 4, slot % 4)
            if slot in scalar_work:
                g, bh = scalar_work[slot]
                interleave_cf(g, bh, "S")
            for step in range(1 if slot < SLOTS else 4):
                while waiting and len(opened) < (4 if slot < SLOTS else 8):
                    m, bh = waiting[0]
                    if max(ready_d[m // MT, 0], ready_c[0, bh]) > slot:
                        break
                    waiting.pop(0)
                    tag = "o"
                    if slot >= SLOTS and spare:
                        tag = "z"
                        spare -= 1
                    acc = psum.tile([P, HALF], F32, name="acc", tag=tag)
                    opened.append([m, bh, 0, acc])
                for tile_ in opened:
                    m, bh, g, acc = tile_
                    h = m // MT
                    if max(ready_d[h, g], ready_c[g, bh]) <= slot:
                        cols = slice(P * (m % MT), P * (m % MT + 1))
                        nc.tensor.matmul_mx(
                            out=acc[:],
                            lhsT=d_q[h, g][:, cols].bitcast(FP8X4),
                            lhsT_scale=d_s[h, g][:, cols],
                            rhs=c_q[g, bh][:].bitcast(FP8X4),
                            rhs_scale=c_s[g, bh][:],
                            start=(g == 0),
                            stop=(g == JG - 1),
                        )
                        tile_[2] += 1
                        if g == JG - 1:
                            opened.remove(tile_)
                            at(slot, -2, drain, m, bh, acc, closed in SHARED_DRAINS)
                            closed += 1
                        break
            for rank, work, args in sorted(vector_work.get(slot, []), key=lambda w: w[0]):
                work(*args)
            slot += 1
